import numpy as np
import ml_dtypes


def mxq(x, axis, fmt="e4m3"):
    dtype, down = {"e4m3": (ml_dtypes.float8_e4m3fn, 7), "e5m2": (ml_dtypes.float8_e5m2, 14)}[fmt]
    v = np.moveaxis(np.asarray(x, np.float32).astype(ml_dtypes.bfloat16).astype(np.float64), axis, -1)
    blocks = v.reshape(v.shape[:-1] + (-1, 32))
    amax = np.abs(blocks).max(-1, keepdims=True)
    byte = np.maximum(np.where(amax > 0, np.frexp(amax)[1] - 1 + 127, 0) - down, 1)
    scale = np.exp2(byte - 127.0)
    codes = (blocks / scale).astype(np.float32).astype(dtype).astype(np.float64)
    return np.moveaxis((codes * scale).reshape(v.shape), -1, axis)


WIDE = False


def mx_kscale(k):
    if not WIDE:
        return np.ones(k)
    levels = np.array([10, -10, 5, -5, 0])
    if k % 512:
        return np.exp2(np.random.permutation(np.resize(levels, k // 32))).repeat(32)
    a = np.empty((k // 512, 16))
    for p in range(k // 512):
        a[p, :8] = np.random.permutation(np.resize(levels, 8))
        for g in range(8):
            far = levels[np.abs(levels - a[p, g]) >= 10]
            a[p, g + 8] = far[np.random.randint(len(far))]
    return np.exp2(a.ravel()).repeat(32)


def f64(x):
    return np.asarray(x).astype(np.float64)


def striped(idx):
    return np.tile(idx.reshape(-1, 16).T, (8, 1)).astype(np.uint16)


def unstriped(offs):
    return offs[:16].T.reshape(-1).astype(np.int64)


def pack_weight(w):
    k, n = w.shape
    w = f64(np.asarray(w, np.float32).astype(ml_dtypes.bfloat16)).reshape(k // 32, 32, n)
    amax = np.abs(w).max(1)
    byte = np.clip(np.where(amax > 0, np.frexp(amax)[1] - 1 + 127 - 7, 1), 1, 254)
    scaled = (w * np.exp2(127.0 - byte)[:, None, :]).reshape(k, n).astype(np.float32)
    words = np.ascontiguousarray(scaled.reshape(k // 512, 128, 4, n).transpose(0, 1, 3, 2)).astype(ml_dtypes.float8_e4m3fn).view(np.uint8)
    return words, np.ascontiguousarray(byte.astype(np.uint8).reshape(k // 512, 16, n))


def unpack_weight(words, scales):
    g, p, n, _ = words.shape
    vals = np.ascontiguousarray(words).view(ml_dtypes.float8_e4m3fn).astype(np.float64) * np.repeat(np.exp2(scales.astype(np.float64) - 127.0), 8, axis=1)[..., None]
    return vals.transpose(0, 1, 3, 2).reshape(g * 512, n)


def planes(y):
    n, m = y.shape
    v = y.astype(np.float32).astype(ml_dtypes.bfloat16).astype(np.float64).reshape(n // 32, 32, m)
    top = np.abs(v).max(1)
    byte = np.clip(np.where(top > 0, np.frexp(top)[1] - 1 + 127 - 7, 1), 1, 254)
    codes = (v * np.exp2(127.0 - byte)[:, None, :]).reshape(n, m).astype(np.float32).astype(ml_dtypes.float8_e4m3fn).view(np.uint8)
    words = codes.reshape(n // 512, 128, 4, m).transpose(0, 1, 3, 2)
    return np.ascontiguousarray(words), np.ascontiguousarray(byte.astype(np.uint8).reshape(n // 512, 16, m))


def sigmoid(v):
    return 1.0 / (1.0 + np.exp(-np.maximum(v, -700.0)))


K, T, S, W, N = 512, 1024, 512, 1024, 512


def setup_inputs():
    n = np.random.standard_normal
    s = mx_kscale(K)[:, None]
    packed_xT = pack_weight(n((K, T)) * s)
    packed_eT = pack_weight(n((K, W)) * s)
    return {
        "x_words": packed_xT[0],
        "x_scales": packed_xT[1],
        "e_words": packed_eT[0],
        "e_scales": packed_eT[1],
        "win": (n((K, N)) / np.sqrt(2 * K) / s).astype(np.float32),
        "vin": (n((K, N)) / np.sqrt(2 * K) / s).astype(np.float32),
        "wfo": (n((K, N)) / np.sqrt(2 * K) / s).astype(np.float32),
        "vfo": (n((K, N)) / np.sqrt(2 * K) / s).astype(np.float32),
        "wex": (n((K, N)) / np.sqrt(2 * K) / s).astype(np.float32),
        "vex": (n((K, N)) / np.sqrt(2 * K) / s).astype(np.float32),
        "wca": (n((K, N)) / np.sqrt(2 * K) / s).astype(np.float32),
        "vca": (n((K, N)) / np.sqrt(2 * K) / s).astype(np.float32),
        "cell": (n((N, T))).astype(np.float32),
        "offs": striped(np.random.permutation(T)[:S]),
        "tok": striped(np.random.permutation(W)[:S]),
    }


def reference(x_words, x_scales, e_words, e_scales, win, vin, wfo, vfo, wex, vex, wca, vca, cell, offs, tok):
    xq = unpack_weight(x_words, x_scales)[:, unstriped(offs)]
    e_tok = unpack_weight(e_words, e_scales)[:, unstriped(tok)]
    b = sigmoid(mxq(f64(wex), 0, "e4m3").T @ xq + mxq(f64(vex), 0, "e4m3").T @ e_tok)
    old = f64(cell)[:, unstriped(offs)]
    f = sigmoid(mxq(f64(wfo), 0, "e4m3").T @ xq + mxq(f64(vfo), 0, "e4m3").T @ e_tok)
    a = sigmoid(mxq(f64(win), 0, "e4m3").T @ xq + mxq(f64(vin), 0, "e4m3").T @ e_tok)
    g = np.tanh(mxq(f64(wca), 0, "e4m3").T @ xq + mxq(f64(vca), 0, "e4m3").T @ e_tok)
    new = old * f + a * g
    out_0 = b * new
    return (out_0,) + planes(out_0)

@@ -1,0 +1,186 @@
+from contextlib import ExitStack
+
+import concourse.mybir as mybir
+
+K, T, S, N = 512, 1024, 512, 512
+FLOPS = 8 * 2 * K * N * S
+
+F32 = mybir.dt.float32
+BF16 = mybir.dt.bfloat16
+I32 = mybir.dt.int32
+U32 = mybir.dt.uint32
+U16 = mybir.dt.uint16
+U8 = mybir.dt.uint8
+FP8X4 = mybir.dt.float8_e4m3fn_x4
+ACT = mybir.ActivationFunctionType
+ALU = mybir.AluOpType
+
+P = 128
+PACK = 4
+HALF = S // 2
+
+
+def tile_picked_zlstm_min_po_kernel(
+    tc, x_words, x_scales, e_words, e_scales, win, vin, wfo, vfo, wex, vex, wca, vca, cell, offs, tok,
+    out_0, out_1, out_2,
+):
+    nc = tc.nc
+    with ExitStack() as ctx:
+        keep = ctx.enter_context(tc.tile_pool(name="keep", bufs=1))
+        ring = ctx.enter_context(tc.tile_pool(name="ring", bufs=4))
+        psum = ctx.enter_context(tc.psum_pool(name="psum", bufs=8))
+
+        def copy_on(engine, out, in_):
+            if engine == "v":
+                nc.vector.tensor_copy(out=out, in_=in_)
+            else:
+                nc.scalar.copy(out=out, in_=in_)
+
+        xs_table = keep.tile([P, T], U8, name="xs_table", align_bytes=64)
+        es_table = keep.tile([P, T], U8, name="es_table", align_bytes=64)
+        warm = keep.tile([P, 8], F32, name="warm")
+        warm_out = keep.tile([P, 8], F32, name="warm_out")
+        nc.gpsimd.memset(xs_table[:].bitcast(I32), 0)
+        nc.gpsimd.memset(es_table[:].bitcast(I32), 0)
+        nc.gpsimd.memset(warm[:], 0.0)
+
+        xw_table = keep.tile([P, T], U32, name="xw_table", align_bytes=64)
+        ew_table = keep.tile([P, T], U32, name="ew_table", align_bytes=64)
+        offs_sb = keep.tile([P, S // 16], U16, name="offs_sb")
+        tok_sb = keep.tile([P, S // 16], U16, name="tok_sb")
+        nc.sync.dma_start(out=xw_table[:].bitcast(I32), in_=x_words[0].rearrange("p n r -> p (n r)").bitcast(I32))
+        nc.sync.dma_start(offs_sb[:], offs)
+        nc.sync.dma_start(out=ew_table[:].bitcast(I32), in_=e_words[0].rearrange("p n r -> p (n r)").bitcast(I32))
+        nc.sync.dma_start(tok_sb[:], tok)
+        for q in range(4):
+            nc.scalar.dma_start(
+                out=xs_table[32 * q : 32 * q + 4, :].bitcast(I32), in_=x_scales[0, 4 * q : 4 * q + 4, :].bitcast(I32)
+            )
+        for q in range(4):
+            nc.gpsimd.dma_start(
+                out=es_table[32 * q : 32 * q + 4, :].bitcast(I32), in_=e_scales[0, 4 * q : 4 * q + 4, :].bitcast(I32)
+            )
+        nc.scalar.activation(out=warm_out[:], in_=warm[:], func=ACT.Sigmoid)
+
+        def load_weight(name, w):
+            raw = keep.tile([P, PACK, N], F32, name="raw_" + name)
+            nc.sync.dma_start(out=raw[:], in_=w.rearrange("(p r) c -> p r c", r=PACK))
+            return raw
+
+        raws = {}
+        for name, w in (("wfo", wfo), ("vfo", vfo), ("win", win), ("vin", vin), ("wca", wca), ("vca", vca)):
+            raws[name] = load_weight(name, w)
+        cells = []
+        for t in range(PACK):
+            rows = keep.tile([P, T], F32, name="cell%d" % t)
+            nc.sync.dma_start(out=rows[:], in_=cell.rearrange("(p t) n -> p t n", t=PACK)[:, t, :])
+            cells.append(rows)
+        for name, w in (("wex", wex), ("vex", vex)):
+            raws[name] = load_weight(name, w)
+
+        def gather(name, table, offsets, dtype):
+            picked = keep.tile([P, S], dtype, name=name, align_bytes=64)
+            nc.vector.tensor_copy(out=picked[:], in_=table[:].indirect(offsets[:]))
+            return picked
+
+        x_codes = gather("x_codes", xw_table, offs_sb, U32)
+        e_codes = gather("e_codes", ew_table, tok_sb, U32)
+        x_plane = gather("x_plane", xs_table, offs_sb, U8)
+        e_plane = gather("e_plane", es_table, tok_sb, U8)
+
+        def quantize_weight(name, engines):
+            pairs = []
+            for u in range(2):
+                grouped = ring.tile([P, 2, P, PACK], BF16, name="grouped", align_bytes=64)
+                copy_on(
+                    engines[u],
+                    grouped[:].rearrange("p t m r -> p m r t"),
+                    raws[name][:].rearrange("p r (m u t) -> p u m r t", u=2, t=2)[:, u],
+                )
+                pairs.append(grouped)
+            made = []
+            for u in range(2):
+                codes = keep.tile([P, 2 * P], U32, name="codes_%s%d" % (name, u), align_bytes=64)
+                plane = keep.tile([P, 2 * P], U8, name="plane_%s%d" % (name, u), align_bytes=64)
+                nc.vector.quantize_mx(
+                    out=codes[:].bitcast(FP8X4), scales=plane[:], in_=pairs[u][:].rearrange("p t m r -> p (t m r)")
+                )
+                made.append((codes, plane))
+            return made
+
+        def passes(banks, weight, codes, plane, first):
+            for t in range(PACK):
+                w_codes, w_plane = weight[t // 2]
+                cols = slice((t % 2) * P, (t % 2 + 1) * P)
+                nc.tensor.matmul_mx(
+                    out=banks[t][:],
+                    lhsT=w_codes[:, cols].bitcast(FP8X4),
+                    lhsT_scale=w_plane[:, cols],
+                    rhs=codes[:].bitcast(FP8X4),
+                    rhs_scale=plane[:],
+                    start=first,
+                    stop=not first,
+                )
+
+        def products(w_name, v_name, w_engines, v_engines):
+            banks = [psum.tile([P, S], F32, name="bank") for t in range(PACK)]
+            passes(banks, quantize_weight(w_name, w_engines), x_codes, x_plane, True)
+            passes(banks, quantize_weight(v_name, v_engines), e_codes, e_plane, False)
+            return banks
+
+        def activate(name, banks, func):
+            values = []
+            for t in range(PACK):
+                value = keep.tile([P, S], F32, name="%s%d" % (name, t))
+                nc.scalar.activation(out=value[:], in_=banks[t][:], func=func)
+                values.append(value)
+            return values
+
+        f = activate("f", products("wfo", "vfo", "ss", "vs"), ACT.Sigmoid)
+        a = activate("a", products("win", "vin", "vs", "vs"), ACT.Sigmoid)
+        g = activate("g", products("wca", "vca", "vs", "vs"), ACT.Tanh)
+
+        new = []
+        for t in range(PACK):
+            kept = keep.tile([P, S], F32, name="kept%d" % t)
+            nc.vector.tensor_tensor(out=kept[:], in0=cells[t][:].indirect(offs_sb[:]), in1=f[t][:], op=ALU.mult)
+            new.append(kept)
+            nc.vector.tensor_tensor(out=a[t][:], in0=a[t][:], in1=g[t][:], op=ALU.mult)
+        b_banks = products("wex", "vex", "ss", "vs")
+        for t in range(PACK):
+            nc.vector.tensor_tensor(out=new[t][:], in0=new[t][:], in1=a[t][:], op=ALU.add)
+
+        y = keep.tile([P, PACK, S], F32, name="y")
+        out_rows = out_0.rearrange("(p t) j -> p t j", t=PACK)
+        for t in range(PACK):
+            b = keep.tile([P, S], F32, name="b%d" % t)
+            pieces = [slice(0, S)] if t < PACK - 1 else [slice(0, HALF), slice(HALF, S)]
+            for cols in pieces:
+                nc.scalar.activation(out=b[:, cols], in_=b_banks[t][:, cols], func=ACT.Sigmoid)
+                nc.vector.tensor_tensor(out=y[:, t, cols], in0=b[:, cols], in1=new[t][:, cols], op=ALU.mult)
+            nc.sync.dma_start(out=out_rows[:, t, :], in_=y[:, t, :])
+
+        y_plane = keep.tile([P, S], U8, name="y_plane", align_bytes=64)
+        words_out = out_1[0].rearrange("p n r -> p (n r)").bitcast(I32)
+        rounded = []
+        for h, engine in enumerate("sv"):
+            cols = slice(h * HALF, (h + 1) * HALF)
+            y_grouped = keep.tile([P, HALF, PACK], BF16, name="y_grouped%d" % h, align_bytes=64)
+            copy_on(
+                engine,
+                y_grouped[:].rearrange("p (c i) t -> p c t i", i=4),
+                y[:, :, cols].rearrange("p t (c i) -> p c t i", i=4),
+            )
+            rounded.append(y_grouped)
+        for h in (1, 0):
+            cols = slice(h * HALF, (h + 1) * HALF)
+            y_codes = keep.tile([P, HALF], U32, name="y_codes%d" % h, align_bytes=64)
+            nc.vector.quantize_mx(
+                out=y_codes[:].bitcast(FP8X4), scales=y_plane[:, cols], in_=rounded[h][:].rearrange("p j t -> p (j t)")
+            )
+            nc.sync.dma_start(out=words_out[:, cols], in_=y_codes[:].bitcast(I32))
+        for q in range(4):
+            queue = nc.sync if q % 2 == 0 else nc.scalar
+            queue.dma_start(
+                out=out_2[0, 4 * q : 4 * q + 4, :].bitcast(I32), in_=y_plane[32 * q : 32 * q + 4, :].bitcast(I32)
+            )

@@ -2,7 +2,10 @@ from contextlib import ExitStack
 
 import concourse.mybir as mybir
 
-K, T, S, N = 512, 1024, 512, 512
+K = 512
+N = 512
+T = 1024
+S = 512
 FLOPS = 8 * 2 * K * N * S
 
 F32 = mybir.dt.float32
@@ -17,7 +20,12 @@ ALU = mybir.AluOpType
 
 P = 128
 PACK = 4
+PAIRS = PACK // 2
+QUADRANTS = 4
 HALF = S // 2
+LINE = 4
+STAGING = 4
+BANKS = 2 * PACK
 
 
 def tile_picked_zlstm_min_po_kernel(
@@ -25,90 +33,89 @@ def tile_picked_zlstm_min_po_kernel(
     out_0, out_1, out_2,
 ):
     nc = tc.nc
+    on_vector = nc.vector.tensor_copy
+    on_scalar = nc.scalar.copy
+
     with ExitStack() as ctx:
         keep = ctx.enter_context(tc.tile_pool(name="keep", bufs=1))
-        ring = ctx.enter_context(tc.tile_pool(name="ring", bufs=4))
-        psum = ctx.enter_context(tc.psum_pool(name="psum", bufs=8))
+        staging = ctx.enter_context(tc.tile_pool(name="staging", bufs=STAGING))
+        psum = ctx.enter_context(tc.psum_pool(name="psum", bufs=BANKS))
 
-        def copy_on(engine, out, in_):
-            if engine == "v":
-                nc.vector.tensor_copy(out=out, in_=in_)
-            else:
-                nc.scalar.copy(out=out, in_=in_)
+        def load_list(name, entries):
+            tile = keep.tile([P, S // 16], U16, name=name)
+            nc.sync.dma_start(tile[:], entries)
+            return tile
 
-        xs_table = keep.tile([P, T], U8, name="xs_table", align_bytes=64)
-        es_table = keep.tile([P, T], U8, name="es_table", align_bytes=64)
-        warm = keep.tile([P, 8], F32, name="warm")
-        warm_out = keep.tile([P, 8], F32, name="warm_out")
-        nc.gpsimd.memset(xs_table[:].bitcast(I32), 0)
-        nc.gpsimd.memset(es_table[:].bitcast(I32), 0)
-        nc.gpsimd.memset(warm[:], 0.0)
+        def load_words(name, words):
+            table = keep.tile([P, T], U32, name=name, align_bytes=64)
+            nc.sync.dma_start(out=table[:].bitcast(I32), in_=words[0].rearrange("p n r -> p (n r)").bitcast(I32))
+            return table
 
-        xw_table = keep.tile([P, T], U32, name="xw_table", align_bytes=64)
-        ew_table = keep.tile([P, T], U32, name="ew_table", align_bytes=64)
-        offs_sb = keep.tile([P, S // 16], U16, name="offs_sb")
-        tok_sb = keep.tile([P, S // 16], U16, name="tok_sb")
-        nc.sync.dma_start(out=xw_table[:].bitcast(I32), in_=x_words[0].rearrange("p n r -> p (n r)").bitcast(I32))
-        nc.sync.dma_start(offs_sb[:], offs)
-        nc.sync.dma_start(out=ew_table[:].bitcast(I32), in_=e_words[0].rearrange("p n r -> p (n r)").bitcast(I32))
-        nc.sync.dma_start(tok_sb[:], tok)
-        for q in range(4):
-            nc.scalar.dma_start(
-                out=xs_table[32 * q : 32 * q + 4, :].bitcast(I32), in_=x_scales[0, 4 * q : 4 * q + 4, :].bitcast(I32)
-            )
-        for q in range(4):
-            nc.gpsimd.dma_start(
-                out=es_table[32 * q : 32 * q + 4, :].bitcast(I32), in_=e_scales[0, 4 * q : 4 * q + 4, :].bitcast(I32)
-            )
-        nc.scalar.activation(out=warm_out[:], in_=warm[:], func=ACT.Sigmoid)
+        def load_plane(name, scales):
+            table = keep.tile([P, T], U8, name=name, align_bytes=64)
+            nc.vector.memset(table[:].bitcast(I32), 0)
+            for q in range(QUADRANTS):
+                nc.sync.dma_start(
+                    out=table[32 * q : 32 * q + 4, :].bitcast(I32), in_=scales[0, 4 * q : 4 * q + 4, :].bitcast(I32)
+                )
+            return table
 
         def load_weight(name, w):
-            raw = keep.tile([P, PACK, N], F32, name="raw_" + name)
+            raw = keep.tile([P, PACK, N], F32, name=name)
             nc.sync.dma_start(out=raw[:], in_=w.rearrange("(p r) c -> p r c", r=PACK))
             return raw
 
-        raws = {}
-        for name, w in (("wfo", wfo), ("vfo", vfo), ("win", win), ("vin", vin), ("wca", wca), ("vca", vca)):
-            raws[name] = load_weight(name, w)
-        cells = []
-        for t in range(PACK):
+        def load_cell(t):
             rows = keep.tile([P, T], F32, name="cell%d" % t)
             nc.sync.dma_start(out=rows[:], in_=cell.rearrange("(p t) n -> p t n", t=PACK)[:, t, :])
-            cells.append(rows)
-        for name, w in (("wex", wex), ("vex", vex)):
-            raws[name] = load_weight(name, w)
+            return rows
 
-        def gather(name, table, offsets, dtype):
+        offs_list = load_list("offs_list", offs)
+        x_word_table = load_words("x_word_table", x_words)
+        tok_list = load_list("tok_list", tok)
+        e_word_table = load_words("e_word_table", e_words)
+        x_plane_table = load_plane("x_plane_table", x_scales)
+        wfo_raw = load_weight("wfo_raw", wfo)
+        e_plane_table = load_plane("e_plane_table", e_scales)
+        vfo_raw = load_weight("vfo_raw", vfo)
+        win_raw = load_weight("win_raw", win)
+        spread_raw, cell_rows = [], []
+        for t, (name, w) in enumerate((("vin_raw", vin), ("wca_raw", wca), ("vca_raw", vca), ("wex_raw", wex))):
+            spread_raw.append(load_weight(name, w))
+            cell_rows.append(load_cell(t))
+        vin_raw, wca_raw, vca_raw, wex_raw = spread_raw
+        vex_raw = load_weight("vex_raw", vex)
+
+        def gather(name, table, entries, dtype):
             picked = keep.tile([P, S], dtype, name=name, align_bytes=64)
-            nc.vector.tensor_copy(out=picked[:], in_=table[:].indirect(offsets[:]))
+            nc.vector.tensor_copy(out=picked[:], in_=table[:].indirect(entries[:]))
             return picked
 
-        x_codes = gather("x_codes", xw_table, offs_sb, U32)
-        e_codes = gather("e_codes", ew_table, tok_sb, U32)
-        x_plane = gather("x_plane", xs_table, offs_sb, U8)
-        e_plane = gather("e_plane", es_table, tok_sb, U8)
+        x_codes = gather("x_codes", x_word_table, offs_list, U32)
+        e_codes = gather("e_codes", e_word_table, tok_list, U32)
+        x_plane = gather("x_plane", x_plane_table, offs_list, U8)
+        e_plane = gather("e_plane", e_plane_table, tok_list, U8)
 
-        def quantize_weight(name, engines):
-            pairs = []
-            for u in range(2):
-                grouped = ring.tile([P, 2, P, PACK], BF16, name="grouped", align_bytes=64)
-                copy_on(
-                    engines[u],
-                    grouped[:].rearrange("p t m r -> p m r t"),
-                    raws[name][:].rearrange("p r (m u t) -> p u m r t", u=2, t=2)[:, u],
+        def quantize_weight(name, raw, copies):
+            rounded = []
+            for u in range(PAIRS):
+                grouped = staging.tile([P, 2, P, PACK], BF16, name="grouped", align_bytes=64)
+                copies[u](
+                    out=grouped[:].rearrange("p t m r -> p m r t"),
+                    in_=raw[:].rearrange("p r (m u t) -> p u m r t", u=PAIRS, t=2)[:, u],
                 )
-                pairs.append(grouped)
-            made = []
-            for u in range(2):
-                codes = keep.tile([P, 2 * P], U32, name="codes_%s%d" % (name, u), align_bytes=64)
-                plane = keep.tile([P, 2 * P], U8, name="plane_%s%d" % (name, u), align_bytes=64)
+                rounded.append(grouped)
+            quantized = []
+            for u in range(PAIRS):
+                codes = keep.tile([P, 2 * P], U32, name="%s_codes%d" % (name, u), align_bytes=64)
+                plane = keep.tile([P, 2 * P], U8, name="%s_plane%d" % (name, u), align_bytes=64)
                 nc.vector.quantize_mx(
-                    out=codes[:].bitcast(FP8X4), scales=plane[:], in_=pairs[u][:].rearrange("p t m r -> p (t m r)")
+                    out=codes[:].bitcast(FP8X4), scales=plane[:], in_=rounded[u][:].rearrange("p t m r -> p (t m r)")
                 )
-                made.append((codes, plane))
-            return made
+                quantized.append((codes, plane))
+            return quantized
 
-        def passes(banks, weight, codes, plane, first):
+        def multiply(banks, weight, codes, plane, first):
             for t in range(PACK):
                 w_codes, w_plane = weight[t // 2]
                 cols = slice((t % 2) * P, (t % 2 + 1) * P)
@@ -122,64 +129,66 @@ def tile_picked_zlstm_min_po_kernel(
                     stop=not first,
                 )
 
-        def products(w_name, v_name, w_engines, v_engines):
+        def products(name, w_raw, w_copies, v_raw, v_copies):
             banks = [psum.tile([P, S], F32, name="bank") for t in range(PACK)]
-            passes(banks, quantize_weight(w_name, w_engines), x_codes, x_plane, True)
-            passes(banks, quantize_weight(v_name, v_engines), e_codes, e_plane, False)
+            multiply(banks, quantize_weight("w" + name, w_raw, w_copies), x_codes, x_plane, True)
+            multiply(banks, quantize_weight("v" + name, v_raw, v_copies), e_codes, e_plane, False)
             return banks
 
         def activate(name, banks, func):
-            values = []
+            pairs = [keep.tile([P, 2, S], F32, name="%s%d" % (name, u)) for u in range(PAIRS)]
+            tiles = [pairs[t // 2][:, t % 2, :] for t in range(PACK)]
             for t in range(PACK):
-                value = keep.tile([P, S], F32, name="%s%d" % (name, t))
-                nc.scalar.activation(out=value[:], in_=banks[t][:], func=func)
-                values.append(value)
-            return values
+                nc.scalar.activation(out=tiles[t], in_=banks[t][:], func=func)
+            return tiles
 
-        f = activate("f", products("wfo", "vfo", "ss", "vs"), ACT.Sigmoid)
-        a = activate("a", products("win", "vin", "vs", "vs"), ACT.Sigmoid)
-        g = activate("g", products("wca", "vca", "vs", "vs"), ACT.Tanh)
+        shared = (on_vector, on_scalar)
+        scalar_alone = (on_scalar, on_scalar)
 
-        new = []
+        forget = activate("forget", products("fo", wfo_raw, scalar_alone, vfo_raw, shared), ACT.Sigmoid)
+        enter_banks = products("in", win_raw, shared, vin_raw, shared)
+
+        new_pairs = [keep.tile([P, 2, S], F32, name="new%d" % u) for u in range(PAIRS)]
+        new = [new_pairs[t // 2][:, t % 2, :] for t in range(PACK)]
         for t in range(PACK):
-            kept = keep.tile([P, S], F32, name="kept%d" % t)
-            nc.vector.tensor_tensor(out=kept[:], in0=cells[t][:].indirect(offs_sb[:]), in1=f[t][:], op=ALU.mult)
-            new.append(kept)
-            nc.vector.tensor_tensor(out=a[t][:], in0=a[t][:], in1=g[t][:], op=ALU.mult)
-        b_banks = products("wex", "vex", "ss", "vs")
-        for t in range(PACK):
-            nc.vector.tensor_tensor(out=new[t][:], in0=new[t][:], in1=a[t][:], op=ALU.add)
+            nc.vector.tensor_tensor(out=new[t], in0=cell_rows[t][:].indirect(offs_list[:]), in1=forget[t], op=ALU.mult)
 
+        enter = activate("enter", enter_banks, ACT.Sigmoid)
+        candidate = activate("candidate", products("ca", wca_raw, shared, vca_raw, shared), ACT.Tanh)
+        exit_banks = products("ex", wex_raw, shared, vex_raw, scalar_alone)
+        for t in range(PACK):
+            nc.vector.tensor_tensor(out=enter[t], in0=enter[t], in1=candidate[t], op=ALU.mult)
+            nc.vector.tensor_tensor(out=new[t], in0=new[t], in1=enter[t], op=ALU.add)
+
+        halves = [slice(0, HALF), slice(HALF, S)]
         y = keep.tile([P, PACK, S], F32, name="y")
         out_rows = out_0.rearrange("(p t) j -> p t j", t=PACK)
         for t in range(PACK):
-            b = keep.tile([P, S], F32, name="b%d" % t)
-            pieces = [slice(0, S)] if t < PACK - 1 else [slice(0, HALF), slice(HALF, S)]
-            for cols in pieces:
-                nc.scalar.activation(out=b[:, cols], in_=b_banks[t][:, cols], func=ACT.Sigmoid)
-                nc.vector.tensor_tensor(out=y[:, t, cols], in0=b[:, cols], in1=new[t][:, cols], op=ALU.mult)
+            gate = keep.tile([P, S], F32, name="exit%d" % t)
+            for cols in halves if t == PACK - 1 else [slice(0, S)]:
+                nc.scalar.activation(out=gate[:, cols], in_=exit_banks[t][:, cols], func=ACT.Sigmoid)
+                nc.vector.tensor_tensor(out=y[:, t, cols], in0=gate[:, cols], in1=new[t][:, cols], op=ALU.mult)
             nc.sync.dma_start(out=out_rows[:, t, :], in_=y[:, t, :])
 
-        y_plane = keep.tile([P, S], U8, name="y_plane", align_bytes=64)
-        words_out = out_1[0].rearrange("p n r -> p (n r)").bitcast(I32)
-        rounded = []
-        for h, engine in enumerate("sv"):
-            cols = slice(h * HALF, (h + 1) * HALF)
+        y_rounded = []
+        for h, copy in enumerate((on_scalar, on_vector)):
             y_grouped = keep.tile([P, HALF, PACK], BF16, name="y_grouped%d" % h, align_bytes=64)
-            copy_on(
-                engine,
-                y_grouped[:].rearrange("p (c i) t -> p c t i", i=4),
-                y[:, :, cols].rearrange("p t (c i) -> p c t i", i=4),
+            copy(
+                out=y_grouped[:].rearrange("p (c i) t -> p c t i", i=LINE),
+                in_=y[:, :, halves[h]].rearrange("p t (c i) -> p c t i", i=LINE),
             )
-            rounded.append(y_grouped)
+            y_rounded.append(y_grouped)
+        y_plane = keep.tile([P, S], U8, name="y_plane", align_bytes=64)
+        out_words = out_1[0].rearrange("p n r -> p (n r)").bitcast(I32)
         for h in (1, 0):
-            cols = slice(h * HALF, (h + 1) * HALF)
             y_codes = keep.tile([P, HALF], U32, name="y_codes%d" % h, align_bytes=64)
             nc.vector.quantize_mx(
-                out=y_codes[:].bitcast(FP8X4), scales=y_plane[:, cols], in_=rounded[h][:].rearrange("p j t -> p (j t)")
+                out=y_codes[:].bitcast(FP8X4),
+                scales=y_plane[:, halves[h]],
+                in_=y_rounded[h][:].rearrange("p j t -> p (j t)"),
             )
-            nc.sync.dma_start(out=words_out[:, cols], in_=y_codes[:].bitcast(I32))
-        for q in range(4):
+            nc.sync.dma_start(out=out_words[:, halves[h]], in_=y_codes[:].bitcast(I32))
+        for q in range(QUADRANTS):
             queue = nc.sync if q % 2 == 0 else nc.scalar
             queue.dma_start(
                 out=out_2[0, 4 * q : 4 * q + 4, :].bitcast(I32), in_=y_plane[32 * q : 32 * q + 4, :].bitcast(I32)

@@ -79,11 +79,12 @@ def tile_picked_zlstm_min_po_kernel(
         e_plane_table = load_plane("e_plane_table", e_scales)
         vfo_raw = load_weight("vfo_raw", vfo)
         win_raw = load_weight("win_raw", win)
-        spread_raw, cell_rows = [], []
-        for t, (name, w) in enumerate((("vin_raw", vin), ("wca_raw", wca), ("vca_raw", vca), ("wex_raw", wex))):
-            spread_raw.append(load_weight(name, w))
-            cell_rows.append(load_cell(t))
-        vin_raw, wca_raw, vca_raw, wex_raw = spread_raw
+        vin_raw = load_weight("vin_raw", vin)
+        cell_rows = [load_cell(t) for t in range(0, 2)]
+        wca_raw = load_weight("wca_raw", wca)
+        vca_raw = load_weight("vca_raw", vca)
+        cell_rows = cell_rows + [load_cell(t) for t in range(2, PACK)]
+        wex_raw = load_weight("wex_raw", wex)
         vex_raw = load_weight("vex_raw", vex)
 
         def gather(name, table, entries, dtype):
@@ -96,10 +97,15 @@ def tile_picked_zlstm_min_po_kernel(
         x_plane = gather("x_plane", x_plane_table, offs_list, U8)
         e_plane = gather("e_plane", e_plane_table, tok_list, U8)
 
+        late_slots = {("wex", 1): "late2", ("vex", 0): "late3"}
+
         def quantize_weight(name, raw, copies):
             rounded = []
             for u in range(PAIRS):
-                grouped = staging.tile([P, 2, P, PACK], BF16, name="grouped", align_bytes=64)
+                if (name, u) in late_slots:
+                    grouped = keep.tile([P, 2, P, PACK], BF16, name="late", tag=late_slots[(name, u)], align_bytes=64)
+                else:
+                    grouped = staging.tile([P, 2, P, PACK], BF16, name="grouped", align_bytes=64)
                 copies[u](
                     out=grouped[:].rearrange("p t m r -> p m r t"),
                     in_=raw[:].rearrange("p r (m u t) -> p u m r t", u=PAIRS, t=2)[:, u],
@@ -144,9 +150,10 @@ def tile_picked_zlstm_min_po_kernel(
 
         shared = (on_vector, on_scalar)
         scalar_alone = (on_scalar, on_scalar)
+        vector_alone = (on_vector, on_vector)
 
         forget = activate("forget", products("fo", wfo_raw, scalar_alone, vfo_raw, shared), ACT.Sigmoid)
-        enter_banks = products("in", win_raw, shared, vin_raw, shared)
+        enter_banks = products("in", win_raw, vector_alone, vin_raw, shared)
 
         new_pairs = [keep.tile([P, 2, S], F32, name="new%d" % u) for u in range(PAIRS)]
         new = [new_pairs[t // 2][:, t % 2, :] for t in range(PACK)]
@@ -154,11 +161,16 @@ def tile_picked_zlstm_min_po_kernel(
             nc.vector.tensor_tensor(out=new[t], in0=cell_rows[t][:].indirect(offs_list[:]), in1=forget[t], op=ALU.mult)
 
         enter = activate("enter", enter_banks, ACT.Sigmoid)
-        candidate = activate("candidate", products("ca", wca_raw, shared, vca_raw, shared), ACT.Tanh)
-        exit_banks = products("ex", wex_raw, shared, vex_raw, scalar_alone)
+        candidate = activate("candidate", products("ca", wca_raw, vector_alone, vca_raw, shared), ACT.Tanh)
+        exit_banks = products("ex", wex_raw, scalar_alone, vex_raw, shared)
         for t in range(PACK):
-            nc.vector.tensor_tensor(out=enter[t], in0=enter[t], in1=candidate[t], op=ALU.mult)
-            nc.vector.tensor_tensor(out=new[t], in0=new[t], in1=enter[t], op=ALU.add)
+            if t < 2:
+                added = enter[t]
+            else:
+                late = keep.tile([P, S], F32, name="added", tag="late%d" % t, align_bytes=64)
+                added = late[:]
+            nc.vector.tensor_tensor(out=added, in0=enter[t], in1=candidate[t], op=ALU.mult)
+            nc.vector.tensor_tensor(out=new[t], in0=new[t], in1=added, op=ALU.add)
 
         halves = [slice(0, HALF), slice(HALF, S)]
         y = keep.tile([P, PACK, S], F32, name="y")

@@ -76,8 +76,8 @@ def tile_picked_zlstm_min_po_kernel(
         e_word_table = load_words("e_word_table", e_words)
         x_plane_table = load_plane("x_plane_table", x_scales)
         wfo_raw = load_weight("wfo_raw", wfo)
-        e_plane_table = load_plane("e_plane_table", e_scales)
         vfo_raw = load_weight("vfo_raw", vfo)
+        e_plane_table = load_plane("e_plane_table", e_scales)
         win_raw = load_weight("win_raw", win)
         vin_raw = load_weight("vin_raw", vin)
         cell_rows = [load_cell(t) for t in range(0, 2)]
@@ -97,18 +97,19 @@ def tile_picked_zlstm_min_po_kernel(
         x_plane = gather("x_plane", x_plane_table, offs_list, U8)
         e_plane = gather("e_plane", e_plane_table, tok_list, U8)
 
-        late_slots = {("wex", 1): "late2", ("vex", 0): "late3"}
+        late_slots = {("wex", 1): "slot_of_tile2", ("vex", 0): "slot_of_tile3"}
 
         def quantize_weight(name, raw, copies):
             rounded = []
             for u in range(PAIRS):
                 if (name, u) in late_slots:
-                    grouped = keep.tile([P, 2, P, PACK], BF16, name="late", tag=late_slots[(name, u)], align_bytes=64)
+                    slot = late_slots[(name, u)]
+                    grouped = keep.tile([P, 2, P, PACK], BF16, name="grouped_late", tag=slot, align_bytes=64)
                 else:
                     grouped = staging.tile([P, 2, P, PACK], BF16, name="grouped", align_bytes=64)
                 copies[u](
-                    out=grouped[:].rearrange("p t m r -> p m r t"),
-                    in_=raw[:].rearrange("p r (m u t) -> p u m r t", u=PAIRS, t=2)[:, u],
+                    out=grouped[:].rearrange("p e m r -> p m r e"),
+                    in_=raw[:].rearrange("p r (m u e) -> p u m r e", u=PAIRS, e=2)[:, u],
                 )
                 rounded.append(grouped)
             quantized = []
@@ -116,7 +117,7 @@ def tile_picked_zlstm_min_po_kernel(
                 codes = keep.tile([P, 2 * P], U32, name="%s_codes%d" % (name, u), align_bytes=64)
                 plane = keep.tile([P, 2 * P], U8, name="%s_plane%d" % (name, u), align_bytes=64)
                 nc.vector.quantize_mx(
-                    out=codes[:].bitcast(FP8X4), scales=plane[:], in_=rounded[u][:].rearrange("p t m r -> p (t m r)")
+                    out=codes[:].bitcast(FP8X4), scales=plane[:], in_=rounded[u][:].rearrange("p e m r -> p (e m r)")
                 )
                 quantized.append((codes, plane))
             return quantized
@@ -152,7 +153,7 @@ def tile_picked_zlstm_min_po_kernel(
         scalar_alone = (on_scalar, on_scalar)
         vector_alone = (on_vector, on_vector)
 
-        forget = activate("forget", products("fo", wfo_raw, scalar_alone, vfo_raw, shared), ACT.Sigmoid)
+        forget = activate("forget", products("fo", wfo_raw, shared, vfo_raw, scalar_alone), ACT.Sigmoid)
         enter_banks = products("in", win_raw, vector_alone, vin_raw, shared)
 
         new_pairs = [keep.tile([P, 2, S], F32, name="new%d" % u) for u in range(PAIRS)]
@@ -163,14 +164,18 @@ def tile_picked_zlstm_min_po_kernel(
         enter = activate("enter", enter_banks, ACT.Sigmoid)
         candidate = activate("candidate", products("ca", wca_raw, vector_alone, vca_raw, shared), ACT.Tanh)
         exit_banks = products("ex", wex_raw, scalar_alone, vex_raw, shared)
-        for t in range(PACK):
-            if t < 2:
-                added = enter[t]
-            else:
-                late = keep.tile([P, S], F32, name="added", tag="late%d" % t, align_bytes=64)
-                added = late[:]
-            nc.vector.tensor_tensor(out=added, in0=enter[t], in1=candidate[t], op=ALU.mult)
-            nc.vector.tensor_tensor(out=new[t], in0=new[t], in1=added, op=ALU.add)
+        for u in range(PAIRS):
+            added = []
+            for t in (2 * u, 2 * u + 1):
+                if u == 0:
+                    product = enter[t]
+                else:
+                    late = keep.tile([P, S], F32, name="added", tag="slot_of_tile%d" % t, align_bytes=64)
+                    product = late[:]
+                nc.vector.tensor_tensor(out=product, in0=enter[t], in1=candidate[t], op=ALU.mult)
+                added.append(product)
+            for t in (2 * u, 2 * u + 1):
+                nc.vector.tensor_tensor(out=new[t], in0=new[t], in1=added[t % 2], op=ALU.add)
 
         halves = [slice(0, HALF), slice(HALF, S)]
         y = keep.tile([P, PACK, S], F32, name="y")

from contextlib import ExitStack

import concourse.mybir as mybir

K = 512
N = 512
T = 1024
S = 512
FLOPS = 8 * 2 * K * N * S

F32 = mybir.dt.float32
BF16 = mybir.dt.bfloat16
I32 = mybir.dt.int32
U32 = mybir.dt.uint32
U16 = mybir.dt.uint16
U8 = mybir.dt.uint8
FP8X4 = mybir.dt.float8_e4m3fn_x4
ACT = mybir.ActivationFunctionType
ALU = mybir.AluOpType

P = 128
PACK = 4
PAIRS = PACK // 2
QUADRANTS = 4
HALF = S // 2
LINE = 4
STAGING = 4
BANKS = 2 * PACK


def tile_picked_zlstm_min_po_kernel(
    tc, x_words, x_scales, e_words, e_scales, win, vin, wfo, vfo, wex, vex, wca, vca, cell, offs, tok,
    out_0, out_1, out_2,
):
    nc = tc.nc
    on_vector = nc.vector.tensor_copy
    on_scalar = nc.scalar.copy

    with ExitStack() as ctx:
        keep = ctx.enter_context(tc.tile_pool(name="keep", bufs=1))
        staging = ctx.enter_context(tc.tile_pool(name="staging", bufs=STAGING))
        psum = ctx.enter_context(tc.psum_pool(name="psum", bufs=BANKS))

        def load_list(name, entries):
            tile = keep.tile([P, S // 16], U16, name=name)
            nc.sync.dma_start(tile[:], entries)
            return tile

        def load_words(name, words):
            table = keep.tile([P, T], U32, name=name, align_bytes=64)
            nc.sync.dma_start(out=table[:].bitcast(I32), in_=words[0].rearrange("p n r -> p (n r)").bitcast(I32))
            return table

        def load_plane(name, scales):
            table = keep.tile([P, T], U8, name=name, align_bytes=64)
            nc.vector.memset(table[:].bitcast(I32), 0)
            for q in range(QUADRANTS):
                nc.sync.dma_start(
                    out=table[32 * q : 32 * q + 4, :].bitcast(I32), in_=scales[0, 4 * q : 4 * q + 4, :].bitcast(I32)
                )
            return table

        def load_weight(name, w):
            raw = keep.tile([P, PACK, N], F32, name=name)
            nc.sync.dma_start(out=raw[:], in_=w.rearrange("(p r) c -> p r c", r=PACK))
            return raw

        def load_cell(t):
            rows = keep.tile([P, T], F32, name="cell%d" % t)
            nc.sync.dma_start(out=rows[:], in_=cell.rearrange("(p t) n -> p t n", t=PACK)[:, t, :])
            return rows

        offs_list = load_list("offs_list", offs)
        x_word_table = load_words("x_word_table", x_words)
        tok_list = load_list("tok_list", tok)
        e_word_table = load_words("e_word_table", e_words)
        x_plane_table = load_plane("x_plane_table", x_scales)
        wfo_raw = load_weight("wfo_raw", wfo)
        vfo_raw = load_weight("vfo_raw", vfo)
        e_plane_table = load_plane("e_plane_table", e_scales)
        win_raw = load_weight("win_raw", win)
        vin_raw = load_weight("vin_raw", vin)
        cell_rows = [load_cell(t) for t in range(0, 2)]
        wca_raw = load_weight("wca_raw", wca)
        vca_raw = load_weight("vca_raw", vca)
        cell_rows = cell_rows + [load_cell(t) for t in range(2, PACK)]
        wex_raw = load_weight("wex_raw", wex)
        vex_raw = load_weight("vex_raw", vex)

        def gather(name, table, entries, dtype):
            picked = keep.tile([P, S], dtype, name=name, align_bytes=64)
            nc.vector.tensor_copy(out=picked[:], in_=table[:].indirect(entries[:]))
            return picked

        x_codes = gather("x_codes", x_word_table, offs_list, U32)
        e_codes = gather("e_codes", e_word_table, tok_list, U32)
        x_plane = gather("x_plane", x_plane_table, offs_list, U8)
        e_plane = gather("e_plane", e_plane_table, tok_list, U8)

        late_slots = {("wex", 1): "slot_of_tile2", ("vex", 0): "slot_of_tile3"}

        def quantize_weight(name, raw, copies):
            rounded = []
            for u in range(PAIRS):
                if (name, u) in late_slots:
                    slot = late_slots[(name, u)]
                    grouped = keep.tile([P, 2, P, PACK], BF16, name="grouped_late", tag=slot, align_bytes=64)
                else:
                    grouped = staging.tile([P, 2, P, PACK], BF16, name="grouped", align_bytes=64)
                copies[u](
                    out=grouped[:].rearrange("p e m r -> p m r e"),
                    in_=raw[:].rearrange("p r (m u e) -> p u m r e", u=PAIRS, e=2)[:, u],
                )
                rounded.append(grouped)
            quantized = []
            for u in range(PAIRS):
                codes = keep.tile([P, 2 * P], U32, name="%s_codes%d" % (name, u), align_bytes=64)
                plane = keep.tile([P, 2 * P], U8, name="%s_plane%d" % (name, u), align_bytes=64)
                nc.vector.quantize_mx(
                    out=codes[:].bitcast(FP8X4), scales=plane[:], in_=rounded[u][:].rearrange("p e m r -> p (e m r)")
                )
                quantized.append((codes, plane))
            return quantized

        def multiply(banks, weight, codes, plane, first):
            for t in range(PACK):
                w_codes, w_plane = weight[t // 2]
                cols = slice((t % 2) * P, (t % 2 + 1) * P)
                nc.tensor.matmul_mx(
                    out=banks[t][:],
                    lhsT=w_codes[:, cols].bitcast(FP8X4),
                    lhsT_scale=w_plane[:, cols],
                    rhs=codes[:].bitcast(FP8X4),
                    rhs_scale=plane[:],
                    start=first,
                    stop=not first,
                )

        def products(name, w_raw, w_copies, v_raw, v_copies):
            banks = [psum.tile([P, S], F32, name="bank") for t in range(PACK)]
            multiply(banks, quantize_weight("w" + name, w_raw, w_copies), x_codes, x_plane, True)
            multiply(banks, quantize_weight("v" + name, v_raw, v_copies), e_codes, e_plane, False)
            return banks

        def activate(name, banks, func):
            pairs = [keep.tile([P, 2, S], F32, name="%s%d" % (name, u)) for u in range(PAIRS)]
            tiles = [pairs[t // 2][:, t % 2, :] for t in range(PACK)]
            for t in range(PACK):
                nc.scalar.activation(out=tiles[t], in_=banks[t][:], func=func)
            return tiles

        shared = (on_vector, on_scalar)
        scalar_alone = (on_scalar, on_scalar)
        vector_alone = (on_vector, on_vector)

        forget = activate("forget", products("fo", wfo_raw, shared, vfo_raw, scalar_alone), ACT.Sigmoid)
        enter_banks = products("in", win_raw, vector_alone, vin_raw, shared)

        new_pairs = [keep.tile([P, 2, S], F32, name="new%d" % u) for u in range(PAIRS)]
        new = [new_pairs[t // 2][:, t % 2, :] for t in range(PACK)]
        for t in range(PACK):
            nc.vector.tensor_tensor(out=new[t], in0=cell_rows[t][:].indirect(offs_list[:]), in1=forget[t], op=ALU.mult)

        enter = activate("enter", enter_banks, ACT.Sigmoid)
        candidate = activate("candidate", products("ca", wca_raw, vector_alone, vca_raw, shared), ACT.Tanh)
        exit_banks = products("ex", wex_raw, scalar_alone, vex_raw, shared)
        for u in range(PAIRS):
            added = []
            for t in (2 * u, 2 * u + 1):
                if u == 0:
                    product = enter[t]
                else:
                    late = keep.tile([P, S], F32, name="added", tag="slot_of_tile%d" % t, align_bytes=64)
                    product = late[:]
                nc.vector.tensor_tensor(out=product, in0=enter[t], in1=candidate[t], op=ALU.mult)
                added.append(product)
            for t in (2 * u, 2 * u + 1):
                nc.vector.tensor_tensor(out=new[t], in0=new[t], in1=added[t % 2], op=ALU.add)

        halves = [slice(0, HALF), slice(HALF, S)]
        y = keep.tile([P, PACK, S], F32, name="y")
        out_rows = out_0.rearrange("(p t) j -> p t j", t=PACK)
        for t in range(PACK):
            gate = keep.tile([P, S], F32, name="exit%d" % t)
            for cols in halves if t == PACK - 1 else [slice(0, S)]:
                nc.scalar.activation(out=gate[:, cols], in_=exit_banks[t][:, cols], func=ACT.Sigmoid)
                nc.vector.tensor_tensor(out=y[:, t, cols], in0=gate[:, cols], in1=new[t][:, cols], op=ALU.mult)
            nc.sync.dma_start(out=out_rows[:, t, :], in_=y[:, t, :])

        y_rounded = []
        for h, copy in enumerate((on_scalar, on_vector)):
            y_grouped = keep.tile([P, HALF, PACK], BF16, name="y_grouped%d" % h, align_bytes=64)
            copy(
                out=y_grouped[:].rearrange("p (c i) t -> p c t i", i=LINE),
                in_=y[:, :, halves[h]].rearrange("p t (c i) -> p c t i", i=LINE),
            )
            y_rounded.append(y_grouped)
        y_plane = keep.tile([P, S], U8, name="y_plane", align_bytes=64)
        out_words = out_1[0].rearrange("p n r -> p (n r)").bitcast(I32)
        for h in (1, 0):
            y_codes = keep.tile([P, HALF], U32, name="y_codes%d" % h, align_bytes=64)
            nc.vector.quantize_mx(
                out=y_codes[:].bitcast(FP8X4),
                scales=y_plane[:, halves[h]],
                in_=y_rounded[h][:].rearrange("p j t -> p (j t)"),
            )
            nc.sync.dma_start(out=out_words[:, halves[h]], in_=y_codes[:].bitcast(I32))
        for q in range(QUADRANTS):
            queue = nc.sync if q % 2 == 0 else nc.scalar
            queue.dma_start(
                out=out_2[0, 4 * q : 4 * q + 4, :].bitcast(I32), in_=y_plane[32 * q : 32 * q + 4, :].bitcast(I32)
            )
